import numpy as np
import ml_dtypes


def mxq(x, axis, fmt="e4m3"):
    dtype, down = {"e4m3": (ml_dtypes.float8_e4m3fn, 7), "e5m2": (ml_dtypes.float8_e5m2, 14)}[fmt]
    v = np.moveaxis(np.asarray(x, np.float32).astype(ml_dtypes.bfloat16).astype(np.float64), axis, -1)
    blocks = v.reshape(v.shape[:-1] + (-1, 32))
    amax = np.abs(blocks).max(-1, keepdims=True)
    byte = np.maximum(np.where(amax > 0, np.frexp(amax)[1] - 1 + 127, 0) - down, 1)
    scale = np.exp2(byte - 127.0)
    codes = (blocks / scale).astype(np.float32).astype(dtype).astype(np.float64)
    return np.moveaxis((codes * scale).reshape(v.shape), -1, axis)


WIDE = False


def mx_kscale(k):
    if not WIDE:
        return np.ones(k)
    levels = np.array([24, -24, 12, -12, 0])
    if k % 512:
        return np.exp2(np.random.permutation(np.resize(levels, k // 32))).repeat(32)
    a = np.empty((k // 512, 16))
    for p in range(k // 512):
        a[p, :8] = np.random.permutation(np.resize(levels, 8))
        for g in range(8):
            far = levels[np.abs(levels - a[p, g]) >= 10]
            a[p, g + 8] = far[np.random.randint(len(far))]
    return np.exp2(a.ravel()).repeat(32)


def f64(x):
    return np.asarray(x).astype(np.float64)


def striped8(idx):
    return np.concatenate([v.reshape(-1, 16).T for v in idx]).astype(np.uint16)


def unstriped8(offs):
    return np.stack([offs[16 * g:16 * g + 16].T.reshape(-1) for g in range(8)]).astype(np.int64)


E2M1 = np.array([0.0, 0.5, 1.0, 1.5, 2.0, 3.0, 4.0, 6.0, -0.0, -0.5, -1.0, -1.5, -2.0, -3.0, -4.0, -6.0])


def pack_weight(w, fmt):
    k, n = w.shape
    w = f64(np.asarray(w, np.float32).astype(ml_dtypes.bfloat16)).reshape(k // 32, 32, n)
    amax = np.abs(w).max(1)
    if fmt == "e4m3":
        byte = np.frexp(amax)[1] - 1 + 127 - 7
    else:
        mant, ex = np.frexp(amax / 6.0)
        byte = np.where(mant > 0.5, ex, ex - 1) + 127
    byte = np.clip(np.where(amax > 0, byte, 1), 1, 254)
    scaled = (w * np.exp2(127.0 - byte)[:, None, :]).reshape(k, n).astype(np.float32)
    by_word = np.ascontiguousarray(scaled.reshape(k // 512, 128, 4, n).transpose(0, 1, 3, 2))
    if fmt == "e4m3":
        words = by_word.astype(ml_dtypes.float8_e4m3fn).view(np.uint8)
    else:
        c = by_word.astype(ml_dtypes.float4_e2m1fn).view(np.uint8) & 0xF
        words = (c[..., 0::2] | (c[..., 1::2] << 4)).reshape(k // 512, 128, 2 * n)
    return np.ascontiguousarray(words), np.ascontiguousarray(byte.astype(np.uint8).reshape(k // 512, 16, n))


def unpack_weight(words, scales, fmt):
    g, _, n = scales.shape
    words = np.ascontiguousarray(words).reshape(g, 128, n, -1)
    if fmt == "e4m3":
        vals = words.view(ml_dtypes.float8_e4m3fn).astype(np.float64)
    else:
        nib = np.empty((g, 128, n, 4), np.uint8)
        nib[..., 0::2] = words & 0xF
        nib[..., 1::2] = words >> 4
        vals = E2M1[nib]
    vals = vals * np.repeat(np.exp2(scales.astype(np.float64) - 127.0), 8, axis=1)[..., None]
    return vals.transpose(0, 1, 3, 2).reshape(g * 512, n)


def split(x):
    m, e = np.frexp(f64(x))
    hi = np.ldexp(np.trunc(16.0 * m) / 16.0, e)
    return hi, f64(x) - hi


def sigm(f):
    return 1.0 / (1.0 + np.exp(-np.maximum(f, -700.0)))


K, N, T, J = 1024, 512, 2048, 1024


def setup_inputs():
    n = np.random.standard_normal
    s = mx_kscale(K)[:, None]
    p_wv = pack_weight(n((K, N)) / np.sqrt(K) / s, "e2m1")
    return {
        "xT": (n((K, T)) * s).astype(np.float32),
        "wgt": np.repeat(np.random.uniform(0.5, 2.0, (8, J)), 16, axis=0).astype(np.float32),
        "wk": (n((K, N)) / np.sqrt(K) / s).astype(np.float32),
        "wv_words": p_wv[0],
        "wv_scales": p_wv[1],
        "st": (n((N, J))).astype(np.float32),
        "offs": striped8(np.stack([np.random.permutation(T)[:J] for _ in range(8)])),
    }


def reference(xT, wgt, wk, wv_words, wv_scales, st, offs):
    idx = unstriped8(offs)
    rows = np.arange(K)
    xg = f64(wgt)[rows // 4 % 128] * f64(xT)[rows[:, None], idx[rows % 512 // 64]]
    xT_ = mxq(xg, 0, "e4m3")
    wk_hi, wk_lo = split(wk)
    wk_hi_, wk_lo_ = mxq(wk_hi, 0, "e4m3"), mxq(wk_lo, 0, "e4m3")
    wv_ = unpack_weight(wv_words, wv_scales, "e2m1")
    ke = wk_hi_.T @ xT_ + wk_lo_.T @ xT_
    ve = wv_.T @ xT_
    gate = sigm(ke * f64(st))
    return gate * ve

@@ -1,0 +1,249 @@
+from contextlib import ExitStack
+
+import concourse.mybir as mybir
+
+K, N, T, J = 1024, 512, 2048, 1024
+FLOPS = 3 * 2 * K * N * J
+
+F32 = mybir.dt.float32
+BF16 = mybir.dt.bfloat16
+I32 = mybir.dt.int32
+U32 = mybir.dt.uint32
+U16 = mybir.dt.uint16
+U8 = mybir.dt.uint8
+FP8X4 = mybir.dt.float8_e4m3fn_x4
+FP4X4 = mybir.dt.float4_e2m1fn_x4
+ALU = mybir.AluOpType
+SIGMOID = mybir.ActivationFunctionType.Sigmoid
+
+P = 128
+PACK = 4
+K_PASS = P * PACK
+PASSES = K // K_PASS
+HALF = 512
+QUARTER = 256
+W_CHUNK = 256
+M_TILES = N // P
+HI_MASK = 0xFFF0FFF0 - (1 << 32)
+HI_MASK_F32 = 0xFFF00000 - (1 << 32)
+
+
+def tile_list_hl_sig_kernel(tc, xT, wgt, wk, wv_words, wv_scales, st, offs, out):
+    nc = tc.nc
+    with ExitStack() as ctx:
+        keep = ctx.enter_context(tc.tile_pool(name="keep", bufs=1))
+        psum = ctx.enter_context(tc.psum_pool(name="psum", bufs=1))
+
+        def sb(name, shape, dtype, tag=None):
+            return keep.tile(shape, dtype, name=name, tag=tag or name, align_bytes=64)
+
+        lists = keep.tile([P, J // 16], U16, name="lists")
+        nc.sync.dma_start(lists[:], offs)
+
+        warm = sb("warm", [P, 2], F32)
+        nc.vector.memset(warm[:, 0:1], 0.0)
+        nc.scalar.activation(warm[:, 1:2], warm[:, 0:1], SIGMOID)
+
+        wv_planes = sb("wv_planes", [P, PASSES, N], U8)
+        nc.gpsimd.memset(wv_planes[:].bitcast(I32), 0)
+        for q in range(4):
+            nc.gpsimd.dma_start(
+                wv_planes[32 * q : 32 * q + 4, :, :].bitcast(I32),
+                wv_scales[:, 4 * q : 4 * q + 4, :].rearrange("a r n -> r a n").bitcast(I32),
+            )
+
+        x_rows = xT.rearrange("(a p t) c -> a t p c", a=PASSES, t=PACK)
+        wk_rows = wk.rearrange("(a p t) n -> a p t n", a=PASSES, t=PACK)
+        x_plane = {}
+        wk_raw = {}
+        w_half = {}
+
+        def load_x(a, t):
+            x_plane[a, t] = sb("x_%d_%d" % (a, t), [P, T], F32)
+            nc.sync.dma_start(x_plane[a, t][:], x_rows[a, t])
+
+        def load_wk(a, c):
+            wk_raw[a, c] = sb("wk_%d_%d" % (a, c), [P, PACK, W_CHUNK], F32)
+            nc.sync.dma_start(wk_raw[a, c][:], wk_rows[a, :, :, c * W_CHUNK : (c + 1) * W_CHUNK])
+
+        def load_wgt(h):
+            w_half[h] = sb("wgt_%d" % h, [P, HALF], F32)
+            nc.sync.dma_start(w_half[h][:], wgt[:, h * HALF : (h + 1) * HALF])
+
+        load_wk(0, 0)
+        load_wk(0, 1)
+        load_wgt(0)
+        load_x(0, 0)
+        load_wgt(1)
+        load_x(0, 1)
+        load_wk(1, 0)
+        load_x(0, 2)
+        load_wk(1, 1)
+        load_x(0, 3)
+        wv_codes = sb("wv_codes", [P, PASSES, 2 * N], U8)
+        nc.sync.dma_start(wv_codes[:].bitcast(I32), wv_words.rearrange("a p b -> p a b").bitcast(I32))
+        for t in range(PACK):
+            load_x(1, t)
+        st_half = {}
+        for h in range(2):
+            st_half[h] = sb("st_%d" % h, [P, M_TILES, HALF], F32)
+            nc.sync.dma_start(st_half[h][:], st.rearrange("(m p) j -> p m j", p=P)[:, :, h * HALF : (h + 1) * HALF])
+
+        def weave(dst, src):
+            nc.scalar.copy(
+                dst.rearrange("p (c i t) -> p c t i", i=4, t=PACK),
+                src.rearrange("p t (c i) -> p c t i", i=4),
+            )
+
+        wk_codes = {}
+        wk_planes = {}
+
+        def split_then_weave(a, c, parts):
+            width = PACK * W_CHUNK
+            raw = wk_raw[a, c]
+            hi = sb("wk_hi_%d_%d" % (a, c), [P, PACK, W_CHUNK], F32)
+            lo = sb("wk_lo_%d_%d" % (a, c), [P, PACK, W_CHUNK], BF16)
+            nc.vector.tensor_scalar(hi[:].bitcast(I32), raw[:].bitcast(I32), HI_MASK_F32, None, ALU.bitwise_and)
+            nc.vector.tensor_tensor(lo[:], raw[:], hi[:], ALU.subtract)
+            weave(parts[:, 0:width], hi[:])
+            weave(parts[:, width : 2 * width], lo[:])
+
+        def weave_then_split(a, c, parts):
+            width = PACK * W_CHUNK
+            woven = sb("wk_woven_%d_%d" % (a, c), [P, width], F32)
+            weave(woven[:], wk_raw[a, c][:])
+            hi = parts[:, 0:width]
+            nc.scalar.copy(hi, woven[:].bitcast(BF16).rearrange("p (w e) -> p w e", e=2)[:, :, 1])
+            nc.vector.tensor_scalar(hi.bitcast(I32), hi.bitcast(I32), HI_MASK, None, ALU.bitwise_and)
+            nc.vector.tensor_tensor(parts[:, width : 2 * width], woven[:], hi, ALU.subtract)
+
+        def split_wk(a, c):
+            parts = sb("wk_parts_%d_%d" % (a, c), [P, 2 * PACK * W_CHUNK], BF16)
+            if a == 0:
+                split_then_weave(a, c, parts)
+            else:
+                weave_then_split(a, c, parts)
+            wk_codes[a, c] = sb("wk_codes_%d_%d" % (a, c), [P, 2 * W_CHUNK], U32)
+            wk_planes[a, c] = sb("wk_planes_%d_%d" % (a, c), [P, 2 * W_CHUNK], U8)
+            nc.vector.quantize_mx(wk_codes[a, c][:].bitcast(FP8X4), wk_planes[a, c][:], parts[:])
+
+        def gather(dst, a, t, j0, width):
+            h = j0 // HALF
+            nc.vector.tensor_tensor(
+                dst,
+                x_plane[a, t][:].indirect(lists[:, j0 // 16 : (j0 + width) // 16]),
+                w_half[h][:, j0 - h * HALF : j0 - h * HALF + width],
+                ALU.mult,
+            )
+
+        xg_codes = {}
+        xg_planes = {}
+
+        def quantise_xg(a, h, woven):
+            xg_codes[a, h] = sb("xg_codes_%d_%d" % (a, h), [P, HALF], U32)
+            xg_planes[a, h] = sb("xg_planes_%d_%d" % (a, h), [P, HALF], U8)
+            nc.vector.quantize_mx(xg_codes[a, h][:].bitcast(FP8X4), xg_planes[a, h][:], woven[:])
+
+        def key_passes(bank, a, h, m):
+            c, col = divmod(m * P, W_CHUNK)
+            for part in range(2):
+                cols = slice(part * W_CHUNK + col, part * W_CHUNK + col + P)
+                nc.tensor.matmul_mx(
+                    bank[:],
+                    lhsT=wk_codes[a, c][:, cols].bitcast(FP8X4),
+                    lhsT_scale=wk_planes[a, c][:, cols],
+                    rhs=xg_codes[a, h][:].bitcast(FP8X4),
+                    rhs_scale=xg_planes[a, h][:],
+                    start=(a == 0 and part == 0),
+                    stop=(a == PASSES - 1 and part == 1),
+                )
+
+        def value_pass(bank, a, h, m):
+            nc.tensor.matmul_mx(
+                bank[:],
+                lhsT=wv_codes[:, a, 2 * P * m : 2 * P * (m + 1)].bitcast(FP4X4),
+                lhsT_scale=wv_planes[:, a, P * m : P * (m + 1)],
+                rhs=xg_codes[a, h][:].bitcast(FP8X4),
+                rhs_scale=xg_planes[a, h][:],
+                start=(a == 0),
+                stop=(a == PASSES - 1),
+            )
+
+        def bank(name, b):
+            return psum.tile([P, HALF], F32, name=name, tag="bank%d" % b)
+
+        picked = {h: sb("picked_0_%d" % h, [P, PACK, HALF], F32) for h in range(2)}
+        split_wk(0, 0)
+        split_wk(0, 1)
+        for t in range(PACK):
+            if t >= 2:
+                split_wk(1, t - 2)
+            for h in range(2):
+                gather(picked[h][:, t, :], 0, t, h * HALF, HALF)
+        for h in range(2):
+            woven = sb("xg_woven_0_%d" % h, [P, PACK * HALF], BF16)
+            weave(woven[:], picked[h][:])
+            quantise_xg(0, h, woven)
+        ke = {(0, m): bank("ke_0_%d" % m, m) for m in range(M_TILES)}
+        ve = {(0, m): bank("ve_0_%d" % m, M_TILES + m) for m in range(M_TILES)}
+        for m in range(M_TILES):
+            key_passes(ke[0, m], 0, 0, m)
+            value_pass(ve[0, m], 0, 0, m)
+
+        def pick_quarter(name, tag, j0, woven):
+            quarter = sb(name, [P, PACK, QUARTER], F32, tag=tag)
+            for t in range(PACK):
+                gather(quarter[:, t, :], 1, t, j0, QUARTER)
+            lo = PACK * (j0 % HALF)
+            weave(woven[:, lo : lo + PACK * QUARTER], quarter[:])
+
+        woven_a = sb("xg_woven_1_0", [P, PACK * HALF], BF16)
+        picked_a = sb("picked_1_0", [P, PACK, HALF], F32)
+        for t in range(PACK - 1):
+            gather(picked_a[:, t, :], 1, t, 0, HALF)
+        for j0 in (0, QUARTER):
+            gather(picked_a[:, PACK - 1, j0 : j0 + QUARTER], 1, PACK - 1, j0, QUARTER)
+            weave(woven_a[:, PACK * j0 : PACK * (j0 + QUARTER)], picked_a[:, :, j0 : j0 + QUARTER])
+        woven_b = sb("xg_woven_1_1", [P, PACK * HALF], BF16)
+        pick_quarter("picked_1_q2", "wgt_0", 2 * QUARTER, woven_b)
+        quantise_xg(1, 0, woven_a)
+        for m in range(M_TILES):
+            value_pass(ve[0, m], 1, 0, m)
+        for m in range(M_TILES):
+            key_passes(ke[0, m], 1, 0, m)
+        pick_quarter("picked_1_q3", "xg_woven_1_0", 3 * QUARTER, woven_b)
+
+        values = {}
+        for m in range(M_TILES):
+            values[m] = sb("values_%d" % m, [P, HALF], F32)
+            nc.scalar.copy(values[m][:], ve[0, m][:])
+            ke[1, m] = bank("ke_1_%d" % m, M_TILES + m)
+            key_passes(ke[1, m], 0, 1, m)
+
+        def gate_of(h, m):
+            logits = sb("logits_%d_%d" % (h, m), [P, HALF], F32)
+            nc.vector.tensor_tensor(logits[:], ke[h, m][:], st_half[h][:, m, :], ALU.mult)
+            nc.scalar.activation(logits[:], logits[:], SIGMOID)
+            return logits
+
+        def finish(h, m, gate, value):
+            nc.vector.tensor_tensor(gate[:], value, gate[:], ALU.mult)
+            nc.sync.dma_start(out[m * P : (m + 1) * P, h * HALF : (h + 1) * HALF], gate[:])
+
+        quantise_xg(1, 1, woven_b)
+        for m in range(M_TILES):
+            key_passes(ke[1, m], 1, 1, m)
+        gates = {}
+        for m in range(M_TILES):
+            gates[0, m] = gate_of(0, m)
+            ve[1, m] = bank("ve_1_%d" % m, m)
+            for a in range(PASSES):
+                value_pass(ve[1, m], a, 1, m)
+        results = sb("results_0", [P, M_TILES, HALF], F32, tag="xg_woven_1_1")
+        for m in range(M_TILES):
+            nc.gpsimd.tensor_tensor(results[:, m, :], values[m][:], gates[0, m][:], ALU.mult)
+            nc.sync.dma_start(out[m * P : (m + 1) * P, 0:HALF], results[:, m, :])
+        for m in range(M_TILES):
+            gates[1, m] = gate_of(1, m)
+        for m in range(M_TILES):
+            finish(1, m, gates[1, m], ve[1, m][:])

@@ -22,10 +22,12 @@ K_PASS = P * PACK
 PASSES = K // K_PASS
 HALF = 512
 QUARTER = 256
-W_CHUNK = 256
 M_TILES = N // P
-HI_MASK = 0xFFF0FFF0 - (1 << 32)
-HI_MASK_F32 = 0xFFF00000 - (1 << 32)
+HI_MASK = 0xFFF00000 - (1 << 32)
+DEFER = 128
+LEAD = 128
+CHUNKS = [256,128]
+ON_GPSIMD = 4
 
 
 def tile_list_hl_sig_kernel(tc, xT, wgt, wk, wv_words, wv_scales, st, offs, out):
@@ -38,56 +40,66 @@ def tile_list_hl_sig_kernel(tc, xT, wgt, wk, wv_words, wv_scales, st, offs, out)
             return keep.tile(shape, dtype, name=name, tag=tag or name, align_bytes=64)
 
         lists = keep.tile([P, J // 16], U16, name="lists")
-        nc.sync.dma_start(lists[:], offs)
 
         warm = sb("warm", [P, 2], F32)
         nc.vector.memset(warm[:, 0:1], 0.0)
         nc.scalar.activation(warm[:, 1:2], warm[:, 0:1], SIGMOID)
 
         wv_planes = sb("wv_planes", [P, PASSES, N], U8)
-        nc.gpsimd.memset(wv_planes[:].bitcast(I32), 0)
-        for q in range(4):
-            nc.gpsimd.dma_start(
-                wv_planes[32 * q : 32 * q + 4, :, :].bitcast(I32),
-                wv_scales[:, 4 * q : 4 * q + 4, :].rearrange("a r n -> r a n").bitcast(I32),
-            )
+        nc.vector.memset(wv_planes[:].bitcast(I32), 0)
 
         x_rows = xT.rearrange("(a p t) c -> a t p c", a=PASSES, t=PACK)
         wk_rows = wk.rearrange("(a p t) n -> a p t n", a=PASSES, t=PACK)
         x_plane = {}
-        wk_raw = {}
+        wk_raw = {a: sb("wk_%d" % a, [P, PACK, N], F32) for a in range(PASSES)}
+        wk_pieces = []
         w_half = {}
 
         def load_x(a, t):
             x_plane[a, t] = sb("x_%d_%d" % (a, t), [P, T], F32)
             nc.sync.dma_start(x_plane[a, t][:], x_rows[a, t])
 
-        def load_wk(a, c):
-            wk_raw[a, c] = sb("wk_%d_%d" % (a, c), [P, PACK, W_CHUNK], F32)
-            nc.sync.dma_start(wk_raw[a, c][:], wk_rows[a, :, :, c * W_CHUNK : (c + 1) * W_CHUNK])
+        def load_wk(a, t0, t1):
+            wk_pieces.append((a, t0, t1))
+            nc.sync.dma_start(wk_raw[a][:, t0:t1, :], wk_rows[a, :, t0:t1, :])
 
         def load_wgt(h):
             w_half[h] = sb("wgt_%d" % h, [P, HALF], F32)
             nc.sync.dma_start(w_half[h][:], wgt[:, h * HALF : (h + 1) * HALF])
 
-        load_wk(0, 0)
-        load_wk(0, 1)
+        load_wk(0, 0, 1)
+        nc.sync.dma_start(lists[:], offs)
+        load_wk(0, 1, 2)
+        load_wk(0, 2, 4)
+        load_wk(1, 0, 2)
+        load_wk(1, 2, 4)
         load_wgt(0)
         load_x(0, 0)
         load_wgt(1)
         load_x(0, 1)
-        load_wk(1, 0)
         load_x(0, 2)
-        load_wk(1, 1)
         load_x(0, 3)
+        load_x(1, 0)
+        load_x(1, 1)
+        load_x(1, 2)
+        load_x(1, 3)
         wv_codes = sb("wv_codes", [P, PASSES, 2 * N], U8)
-        nc.sync.dma_start(wv_codes[:].bitcast(I32), wv_words.rearrange("a p b -> p a b").bitcast(I32))
-        for t in range(PACK):
-            load_x(1, t)
-        st_half = {}
-        for h in range(2):
-            st_half[h] = sb("st_%d" % h, [P, M_TILES, HALF], F32)
-            nc.sync.dma_start(st_half[h][:], st.rearrange("(m p) j -> p m j", p=P)[:, :, h * HALF : (h + 1) * HALF])
+
+        def load_wv():
+            nc.sync.dma_start(wv_codes[:].bitcast(I32), wv_words.rearrange("a p b -> p a b").bitcast(I32))
+            for q in range(4):
+                nc.sync.dma_start(
+                    wv_planes[32 * q : 32 * q + 4, :, :].bitcast(I32),
+                    wv_scales[:, 4 * q : 4 * q + 4, :].rearrange("a r n -> r a n").bitcast(I32),
+                )
+
+        load_wv()
+        st_rows = {}
+        for m in range(M_TILES):
+            st_rows[m] = sb("st_%d" % m, [P, J], F32)
+            nc.sync.dma_start(st_rows[m][:], st[m * P : (m + 1) * P, :])
+            if m == -1:
+                load_wv()
 
         def weave(dst, src):
             nc.scalar.copy(
@@ -95,37 +107,26 @@ def tile_list_hl_sig_kernel(tc, xT, wgt, wk, wv_words, wv_scales, st, offs, out)
                 src.rearrange("p t (c i) -> p c t i", i=4),
             )
 
+        wk_hi = {a: sb("wk_hi_%d" % a, [P, PACK, N], F32) for a in range(PASSES)}
+        wk_lo = {a: sb("wk_lo_%d" % a, [P, PACK, N], BF16) for a in range(PASSES)}
         wk_codes = {}
         wk_planes = {}
 
-        def split_then_weave(a, c, parts):
-            width = PACK * W_CHUNK
-            raw = wk_raw[a, c]
-            hi = sb("wk_hi_%d_%d" % (a, c), [P, PACK, W_CHUNK], F32)
-            lo = sb("wk_lo_%d_%d" % (a, c), [P, PACK, W_CHUNK], BF16)
-            nc.vector.tensor_scalar(hi[:].bitcast(I32), raw[:].bitcast(I32), HI_MASK_F32, None, ALU.bitwise_and)
-            nc.vector.tensor_tensor(lo[:], raw[:], hi[:], ALU.subtract)
-            weave(parts[:, 0:width], hi[:])
-            weave(parts[:, width : 2 * width], lo[:])
+        def split_wk(a):
+            for b, t0, t1 in wk_pieces:
+                if b == a:
+                    raw = wk_raw[a][:, t0:t1, :]
+                    hi = wk_hi[a][:, t0:t1, :]
+                    nc.vector.tensor_scalar(hi.bitcast(I32), raw.bitcast(I32), HI_MASK, None, ALU.bitwise_and)
+                    nc.vector.tensor_tensor(wk_lo[a][:, t0:t1, :], raw, hi, ALU.subtract)
 
-        def weave_then_split(a, c, parts):
-            width = PACK * W_CHUNK
-            woven = sb("wk_woven_%d_%d" % (a, c), [P, width], F32)
-            weave(woven[:], wk_raw[a, c][:])
-            hi = parts[:, 0:width]
-            nc.scalar.copy(hi, woven[:].bitcast(BF16).rearrange("p (w e) -> p w e", e=2)[:, :, 1])
-            nc.vector.tensor_scalar(hi.bitcast(I32), hi.bitcast(I32), HI_MASK, None, ALU.bitwise_and)
-            nc.vector.tensor_tensor(parts[:, width : 2 * width], woven[:], hi, ALU.subtract)
-
-        def split_wk(a, c):
-            parts = sb("wk_parts_%d_%d" % (a, c), [P, 2 * PACK * W_CHUNK], BF16)
-            if a == 0:
-                split_then_weave(a, c, parts)
-            else:
-                weave_then_split(a, c, parts)
-            wk_codes[a, c] = sb("wk_codes_%d_%d" % (a, c), [P, 2 * W_CHUNK], U32)
-            wk_planes[a, c] = sb("wk_planes_%d_%d" % (a, c), [P, 2 * W_CHUNK], U8)
-            nc.vector.quantize_mx(wk_codes[a, c][:].bitcast(FP8X4), wk_planes[a, c][:], parts[:])
+        def quantise_wk(a, tags):
+            for part, src in enumerate((wk_hi[a], wk_lo[a])):
+                woven_part = sb("wk_woven_%d_%d" % (a, part), [P, PACK * N], BF16)
+                weave(woven_part[:], src[:])
+                wk_codes[a, part] = sb("wk_codes_%d_%d" % (a, part), [P, N], U32, tag=tags[part])
+                wk_planes[a, part] = sb("wk_planes_%d_%d" % (a, part), [P, N], U8)
+                nc.vector.quantize_mx(wk_codes[a, part][:].bitcast(FP8X4), wk_planes[a, part][:], woven_part[:])
 
         def gather(dst, a, t, j0, width):
             h = j0 // HALF
@@ -139,19 +140,18 @@ def tile_list_hl_sig_kernel(tc, xT, wgt, wk, wv_words, wv_scales, st, offs, out)
         xg_codes = {}
         xg_planes = {}
 
-        def quantise_xg(a, h, woven):
-            xg_codes[a, h] = sb("xg_codes_%d_%d" % (a, h), [P, HALF], U32)
+        def quantise_xg(a, h, tag=None):
+            xg_codes[a, h] = sb("xg_codes_%d_%d" % (a, h), [P, HALF], U32, tag=tag)
             xg_planes[a, h] = sb("xg_planes_%d_%d" % (a, h), [P, HALF], U8)
-            nc.vector.quantize_mx(xg_codes[a, h][:].bitcast(FP8X4), xg_planes[a, h][:], woven[:])
+            nc.vector.quantize_mx(xg_codes[a, h][:].bitcast(FP8X4), xg_planes[a, h][:], woven[a, h][:])
 
         def key_passes(bank, a, h, m):
-            c, col = divmod(m * P, W_CHUNK)
+            cols = slice(m * P, (m + 1) * P)
             for part in range(2):
-                cols = slice(part * W_CHUNK + col, part * W_CHUNK + col + P)
                 nc.tensor.matmul_mx(
                     bank[:],
-                    lhsT=wk_codes[a, c][:, cols].bitcast(FP8X4),
-                    lhsT_scale=wk_planes[a, c][:, cols],
+                    lhsT=wk_codes[a, part][:, cols].bitcast(FP8X4),
+                    lhsT_scale=wk_planes[a, part][:, cols],
                     rhs=xg_codes[a, h][:].bitcast(FP8X4),
                     rhs_scale=xg_planes[a, h][:],
                     start=(a == 0 and part == 0),
@@ -169,81 +169,101 @@ def tile_list_hl_sig_kernel(tc, xT, wgt, wk, wv_words, wv_scales, st, offs, out)
                 stop=(a == PASSES - 1),
             )
 
-        def bank(name, b):
+        def psum_bank(name, b):
             return psum.tile([P, HALF], F32, name=name, tag="bank%d" % b)
 
-        picked = {h: sb("picked_0_%d" % h, [P, PACK, HALF], F32) for h in range(2)}
-        split_wk(0, 0)
-        split_wk(0, 1)
+        def pick(picked, a, j0, width):
+            for t in range(PACK):
+                gather(picked[:, t, :], a, t, j0, width)
+            lo = PACK * (j0 % HALF)
+            weave(woven[a, j0 // HALF][:, lo : lo + PACK * width], picked)
+
+        woven = {(a, h): sb("xg_woven_%d_%d" % (a, h), [P, PACK * HALF], BF16) for a in range(PASSES) for h in range(2)}
+
+        picked_00 = sb("picked_0_0", [P, PACK, HALF], F32)
+        picked_01 = sb("picked_0_1", [P, PACK, HALF - DEFER], F32)
+        split_wk(0)
         for t in range(PACK):
-            if t >= 2:
-                split_wk(1, t - 2)
-            for h in range(2):
-                gather(picked[h][:, t, :], 0, t, h * HALF, HALF)
-        for h in range(2):
-            woven = sb("xg_woven_0_%d" % h, [P, PACK * HALF], BF16)
-            weave(woven[:], picked[h][:])
-            quantise_xg(0, h, woven)
-        ke = {(0, m): bank("ke_0_%d" % m, m) for m in range(M_TILES)}
-        ve = {(0, m): bank("ve_0_%d" % m, M_TILES + m) for m in range(M_TILES)}
+            gather(picked_00[:, t, :], 0, t, 0, HALF)
+            gather(picked_01[:, t, :], 0, t, HALF, HALF - DEFER)
+        split_wk(1)
+        quantise_wk(0, (None, None))
+        quantise_wk(1, (None, None))
+        weave(woven[0, 0][:], picked_00[:])
+        quantise_xg(0, 0)
+        weave(woven[0, 1][:, 0 : PACK * (HALF - DEFER)], picked_01[:])
+        ke = {(0, m): psum_bank("ke_0_%d" % m, m) for m in range(M_TILES)}
+        ve = {(0, m): psum_bank("ve_0_%d" % m, M_TILES + m) for m in range(M_TILES)}
         for m in range(M_TILES):
             key_passes(ke[0, m], 0, 0, m)
+        for m in range(M_TILES):
             value_pass(ve[0, m], 0, 0, m)
 
-        def pick_quarter(name, tag, j0, woven):
-            quarter = sb(name, [P, PACK, QUARTER], F32, tag=tag)
-            for t in range(PACK):
-                gather(quarter[:, t, :], 1, t, j0, QUARTER)
-            lo = PACK * (j0 % HALF)
-            weave(woven[:, lo : lo + PACK * QUARTER], quarter[:])
-
-        woven_a = sb("xg_woven_1_0", [P, PACK * HALF], BF16)
-        picked_a = sb("picked_1_0", [P, PACK, HALF], F32)
+        picked_10 = sb("picked_1_0", [P, PACK, HALF], F32)
         for t in range(PACK - 1):
-            gather(picked_a[:, t, :], 1, t, 0, HALF)
+            gather(picked_10[:, t, :], 1, t, 0, HALF)
         for j0 in (0, QUARTER):
-            gather(picked_a[:, PACK - 1, j0 : j0 + QUARTER], 1, PACK - 1, j0, QUARTER)
-            weave(woven_a[:, PACK * j0 : PACK * (j0 + QUARTER)], picked_a[:, :, j0 : j0 + QUARTER])
-        woven_b = sb("xg_woven_1_1", [P, PACK * HALF], BF16)
-        pick_quarter("picked_1_q2", "wgt_0", 2 * QUARTER, woven_b)
-        quantise_xg(1, 0, woven_a)
+            gather(picked_10[:, PACK - 1, j0 : j0 + QUARTER], 1, PACK - 1, j0, QUARTER)
+            weave(woven[1, 0][:, PACK * j0 : PACK * (j0 + QUARTER)], picked_10[:, :, j0 : j0 + QUARTER])
+        held = sb("picked_held", [P, PACK * (DEFER + LEAD)], F32, tag="wgt_0")
+        pick(held[:, 0 : PACK * DEFER].rearrange("p (t c) -> p t c", t=PACK), 0, J - DEFER, DEFER)
+        pick(held[:, PACK * DEFER :].rearrange("p (t c) -> p t c", t=PACK), 1, HALF, LEAD)
+        quantise_xg(1, 0)
         for m in range(M_TILES):
             value_pass(ve[0, m], 1, 0, m)
         for m in range(M_TILES):
             key_passes(ke[0, m], 1, 0, m)
-        pick_quarter("picked_1_q3", "xg_woven_1_0", 3 * QUARTER, woven_b)
-
+        quantise_xg(0, 1)
         values = {}
         for m in range(M_TILES):
             values[m] = sb("values_%d" % m, [P, HALF], F32)
             nc.scalar.copy(values[m][:], ve[0, m][:])
-            ke[1, m] = bank("ke_1_%d" % m, M_TILES + m)
+            ke[1, m] = psum_bank("ke_1_%d" % m, M_TILES + m)
             key_passes(ke[1, m], 0, 1, m)
+        picked_11 = sb("picked_1_1", [P, PACK * (HALF - LEAD)], F32, tag="xg_woven_1_0")
+        j0 = HALF + LEAD
+        for width in CHUNKS:
+            lo = PACK * (j0 - HALF - LEAD)
+            pick(picked_11[:, lo : lo + PACK * width].rearrange("p (t c) -> p t c", t=PACK), 1, j0, width)
+            j0 = j0 + width
 
-        def gate_of(h, m):
-            logits = sb("logits_%d_%d" % (h, m), [P, HALF], F32)
-            nc.vector.tensor_tensor(logits[:], ke[h, m][:], st_half[h][:, m, :], ALU.mult)
+        def gate_of(h, m, logits):
+            nc.vector.tensor_tensor(logits[:], ke[h, m][:], st_rows[m][:, h * HALF : (h + 1) * HALF], ALU.mult)
             nc.scalar.activation(logits[:], logits[:], SIGMOID)
             return logits
 
         def finish(h, m, gate, value):
-            nc.vector.tensor_tensor(gate[:], value, gate[:], ALU.mult)
-            nc.sync.dma_start(out[m * P : (m + 1) * P, h * HALF : (h + 1) * HALF], gate[:])
+            if m < 0:
+                staged = sb("values_1_%d" % m, [P, HALF], F32)
+                nc.scalar.copy(staged[:], value[:])
+                nc.gpsimd.tensor_tensor(gate[:], staged[:], gate[:], ALU.mult)
+                nc.sync.dma_start(out[m * P : (m + 1) * P, h * HALF : (h + 1) * HALF], gate[:])
+            else:
+                step = 512 if m == M_TILES - 1 else HALF
+                for c0 in range(0, HALF, step):
+                    cols = slice(c0, c0 + step)
+                    nc.vector.tensor_tensor(gate[:, cols], value[:, cols], gate[:, cols], ALU.mult)
+                    nc.sync.dma_start(out[m * P : (m + 1) * P, h * HALF + c0 : h * HALF + c0 + step], gate[:, cols])
 
-        quantise_xg(1, 1, woven_b)
-        for m in range(M_TILES):
-            key_passes(ke[1, m], 1, 1, m)
+        quantise_xg(1, 1)
+        late = sb("late", [P, M_TILES + 2, HALF], F32, tag="xg_woven_1_1")
         gates = {}
         for m in range(M_TILES):
-            gates[0, m] = gate_of(0, m)
-            ve[1, m] = bank("ve_1_%d" % m, m)
-            for a in range(PASSES):
-                value_pass(ve[1, m], a, 1, m)
-        results = sb("results_0", [P, M_TILES, HALF], F32, tag="xg_woven_1_1")
+            if m < M_TILES - 2:
+                gates[0, m] = gate_of(0, m, sb("logits_0_%d" % m, [P, HALF], F32))
+            else:
+                gates[0, m] = gate_of(0, m, late[:, m + 2, :])
         for m in range(M_TILES):
-            nc.gpsimd.tensor_tensor(results[:, m, :], values[m][:], gates[0, m][:], ALU.mult)
-            nc.sync.dma_start(out[m * P : (m + 1) * P, 0:HALF], results[:, m, :])
+            ve[1, m] = psum_bank("ve_1_%d" % m, m)
         for m in range(M_TILES):
-            gates[1, m] = gate_of(1, m)
-        for m in range(M_TILES):
-            finish(1, m, gates[1, m], ve[1, m][:])
+            nc.gpsimd.tensor_tensor(late[:, m, :], values[m][:], gates[0, m][:], ALU.mult)
+            nc.sync.dma_start(out[m * P : (m + 1) * P, 0:HALF], late[:, m, :])
+        for m in range(M_TILES + 2):
+            if m < M_TILES:
+                key_passes(ke[1, m], 1, 1, m)
+                gates[1, m] = gate_of(1, m, sb("logits_1_%d" % m, [P, HALF], F32))
+            if m >= 2:
+                done = m - 2
+                for a in range(PASSES):
+                    value_pass(ve[1, done], a, 1, done)
+                finish(1, done, gates[1, done], ve[1, done])

@@ -1,6 +1,7 @@
 from contextlib import ExitStack
 
 import concourse.mybir as mybir
+from concourse.masks import make_identity
 
 K, N, T, J = 1024, 512, 2048, 1024
 FLOPS = 3 * 2 * K * N * J
@@ -14,20 +15,25 @@ U8 = mybir.dt.uint8
 FP8X4 = mybir.dt.float8_e4m3fn_x4
 FP4X4 = mybir.dt.float4_e2m1fn_x4
 ALU = mybir.AluOpType
-SIGMOID = mybir.ActivationFunctionType.Sigmoid
+ACT = mybir.ActivationFunctionType
 
 P = 128
-PACK = 4
-K_PASS = P * PACK
+SLOTS = 4
+K_PASS = P * SLOTS
 PASSES = K // K_PASS
 HALF = 512
-QUARTER = 256
+QUARTER = HALF // 2
 M_TILES = N // P
+LIST_ROWS = 16
+HI, LO = 0, 1
+
 HI_MASK = 0xFFF00000 - (1 << 32)
-DEFER = 128
-LEAD = 128
-CHUNKS = [256,128]
-ON_GPSIMD = 4
+SIGN_BIT = -(1 << 31)
+
+RUN_BESIDE_WEAVE = 192
+RUNS_AFTER_QUANTISE = (192, 128)
+GATES_BEHIND_LAST_QUANTISE = 2
+FINISH_LAG = 2
 
 
 def tile_list_hl_sig_kernel(tc, xT, wgt, wk, wv_words, wv_scales, st, offs, out):
@@ -36,234 +42,246 @@ def tile_list_hl_sig_kernel(tc, xT, wgt, wk, wv_words, wv_scales, st, offs, out)
         keep = ctx.enter_context(tc.tile_pool(name="keep", bufs=1))
         psum = ctx.enter_context(tc.psum_pool(name="psum", bufs=1))
 
-        def sb(name, shape, dtype, tag=None):
+        def sbuf_tile(name, shape, dtype, tag=None):
             return keep.tile(shape, dtype, name=name, tag=tag or name, align_bytes=64)
 
-        lists = keep.tile([P, J // 16], U16, name="lists")
+        def psum_tile(name, bank, shape):
+            return psum.tile(shape, F32, name=name, tag="bank%d" % bank)
 
-        warm = sb("warm", [P, 2], F32)
+        lists = keep.tile([P, J // LIST_ROWS], U16, name="lists")
+
+        warm = sbuf_tile("warm", [P, 2], F32)
         nc.vector.memset(warm[:, 0:1], 0.0)
-        nc.scalar.activation(warm[:, 1:2], warm[:, 0:1], SIGMOID)
+        nc.scalar.activation(warm[:, 1:2], warm[:, 0:1], ACT.Sigmoid)
 
-        wv_planes = sb("wv_planes", [P, PASSES, N], U8)
-        nc.vector.memset(wv_planes[:].bitcast(I32), 0)
+        wv_scale_tile = sbuf_tile("wv_scale_tile", [P, PASSES, N], U8)
+        nc.vector.memset(wv_scale_tile[:].bitcast(I32), 0)
 
-        x_rows = xT.rearrange("(a p t) c -> a t p c", a=PASSES, t=PACK)
-        wk_rows = wk.rearrange("(a p t) n -> a p t n", a=PASSES, t=PACK)
-        x_plane = {}
-        wk_raw = {a: sb("wk_%d" % a, [P, PACK, N], F32) for a in range(PASSES)}
-        wk_pieces = []
-        w_half = {}
+        x_rows = xT.rearrange("(a p t) c -> a t p c", a=PASSES, t=SLOTS)
+        wk_rows = wk.rearrange("(a p t) n -> a p t n", a=PASSES, t=SLOTS)
+        x_tile = {}
+        wk_raw = {a: sbuf_tile("wk_raw_%d" % a, [P, SLOTS, N], F32) for a in range(PASSES)}
+        wgt_half = {}
+        slot_pairs = (slice(0, 2), slice(2, 4))
 
         def load_x(a, t):
-            x_plane[a, t] = sb("x_%d_%d" % (a, t), [P, T], F32)
-            nc.sync.dma_start(x_plane[a, t][:], x_rows[a, t])
-
-        def load_wk(a, t0, t1):
-            wk_pieces.append((a, t0, t1))
-            nc.sync.dma_start(wk_raw[a][:, t0:t1, :], wk_rows[a, :, t0:t1, :])
+            x_tile[a, t] = sbuf_tile("x_%d_%d" % (a, t), [P, T], F32)
+            nc.sync.dma_start(x_tile[a, t][:], x_rows[a, t])
 
         def load_wgt(h):
-            w_half[h] = sb("wgt_%d" % h, [P, HALF], F32)
-            nc.sync.dma_start(w_half[h][:], wgt[:, h * HALF : (h + 1) * HALF])
+            wgt_half[h] = sbuf_tile("wgt_%d" % h, [P, HALF], F32)
+            nc.sync.dma_start(wgt_half[h][:], wgt[:, h * HALF : (h + 1) * HALF])
 
-        load_wk(0, 0, 1)
+        nc.sync.dma_start(wk_raw[0][:, slot_pairs[0], :], wk_rows[0, :, slot_pairs[0], :])
         nc.sync.dma_start(lists[:], offs)
-        load_wk(0, 1, 2)
-        load_wk(0, 2, 4)
-        load_wk(1, 0, 2)
-        load_wk(1, 2, 4)
+        nc.sync.dma_start(wk_raw[0][:, slot_pairs[1], :], wk_rows[0, :, slot_pairs[1], :])
         load_wgt(0)
         load_x(0, 0)
         load_wgt(1)
-        load_x(0, 1)
-        load_x(0, 2)
-        load_x(0, 3)
-        load_x(1, 0)
-        load_x(1, 1)
-        load_x(1, 2)
-        load_x(1, 3)
-        wv_codes = sb("wv_codes", [P, PASSES, 2 * N], U8)
+        nc.sync.dma_start(wk_raw[1][:], wk_rows[1])
+        for k_tile in range(1, PASSES * SLOTS):
+            load_x(*divmod(k_tile, SLOTS))
 
-        def load_wv():
-            nc.sync.dma_start(wv_codes[:].bitcast(I32), wv_words.rearrange("a p b -> p a b").bitcast(I32))
-            for q in range(4):
-                nc.sync.dma_start(
-                    wv_planes[32 * q : 32 * q + 4, :, :].bitcast(I32),
-                    wv_scales[:, 4 * q : 4 * q + 4, :].rearrange("a r n -> r a n").bitcast(I32),
-                )
-
-        load_wv()
-        st_rows = {}
+        wv_codes = sbuf_tile("wv_codes", [P, PASSES, 2 * N], U8)
+        nc.sync.dma_start(wv_codes[:].bitcast(I32), wv_words.rearrange("a p b -> p a b").bitcast(I32))
+        for quadrant in range(4):
+            nc.sync.dma_start(
+                wv_scale_tile[32 * quadrant : 32 * quadrant + 4, :, :].bitcast(I32),
+                wv_scales[:, 4 * quadrant : 4 * quadrant + 4, :].rearrange("a r n -> r a n").bitcast(I32),
+            )
+        st_tile = {}
         for m in range(M_TILES):
-            st_rows[m] = sb("st_%d" % m, [P, J], F32)
-            nc.sync.dma_start(st_rows[m][:], st[m * P : (m + 1) * P, :])
-            if m == -1:
-                load_wv()
+            st_tile[m] = sbuf_tile("st_%d" % m, [P, J], F32)
+            nc.sync.dma_start(st_tile[m][:], st[m * P : (m + 1) * P, :])
+
+        def woven_view(dst):
+            return dst.rearrange("p (c i t) -> p c t i", i=4, t=SLOTS)
+
+        def slotted_view(src):
+            return src.rearrange("p t (c i) -> p c t i", i=4)
 
         def weave(dst, src):
-            nc.scalar.copy(
-                dst.rearrange("p (c i t) -> p c t i", i=4, t=PACK),
-                src.rearrange("p t (c i) -> p c t i", i=4),
-            )
+            nc.scalar.copy(woven_view(dst), slotted_view(src))
 
-        wk_hi = {a: sb("wk_hi_%d" % a, [P, PACK, N], F32) for a in range(PASSES)}
-        wk_lo = {a: sb("wk_lo_%d" % a, [P, PACK, N], BF16) for a in range(PASSES)}
-        wk_codes = {}
-        wk_planes = {}
-
-        def split_wk(a):
-            for b, t0, t1 in wk_pieces:
-                if b == a:
-                    raw = wk_raw[a][:, t0:t1, :]
-                    hi = wk_hi[a][:, t0:t1, :]
-                    nc.vector.tensor_scalar(hi.bitcast(I32), raw.bitcast(I32), HI_MASK, None, ALU.bitwise_and)
-                    nc.vector.tensor_tensor(wk_lo[a][:, t0:t1, :], raw, hi, ALU.subtract)
-
-        def quantise_wk(a, tags):
-            for part, src in enumerate((wk_hi[a], wk_lo[a])):
-                woven_part = sb("wk_woven_%d_%d" % (a, part), [P, PACK * N], BF16)
-                weave(woven_part[:], src[:])
-                wk_codes[a, part] = sb("wk_codes_%d_%d" % (a, part), [P, N], U32, tag=tags[part])
-                wk_planes[a, part] = sb("wk_planes_%d_%d" % (a, part), [P, N], U8)
-                nc.vector.quantize_mx(wk_codes[a, part][:].bitcast(FP8X4), wk_planes[a, part][:], woven_part[:])
+        def quantise(name, woven_tile, tag=None):
+            width = woven_tile.shape[1] // SLOTS
+            codes = sbuf_tile(name + "_codes", [P, width], U32, tag=tag)
+            scales = sbuf_tile(name + "_scales", [P, width], U8)
+            nc.vector.quantize_mx(codes[:].bitcast(FP8X4), scales[:], woven_tile[:])
+            return codes, scales
 
         def gather(dst, a, t, j0, width):
-            h = j0 // HALF
+            h, c0 = divmod(j0, HALF)
             nc.vector.tensor_tensor(
                 dst,
-                x_plane[a, t][:].indirect(lists[:, j0 // 16 : (j0 + width) // 16]),
-                w_half[h][:, j0 - h * HALF : j0 - h * HALF + width],
+                x_tile[a, t][:].indirect(lists[:, j0 // LIST_ROWS : (j0 + width) // LIST_ROWS]),
+                wgt_half[h][:, c0 : c0 + width],
                 ALU.mult,
             )
 
-        xg_codes = {}
-        xg_planes = {}
+        def gather_and_weave(flat, a, j0, width):
+            picked = flat.rearrange("p (t c) -> p t c", t=SLOTS)
+            for t in range(SLOTS):
+                gather(picked[:, t, :], a, t, j0, width)
+            h, c0 = divmod(j0, HALF)
+            weave(xg_woven[a, h][:, SLOTS * c0 : SLOTS * (c0 + width)], picked)
 
-        def quantise_xg(a, h, tag=None):
-            xg_codes[a, h] = sb("xg_codes_%d_%d" % (a, h), [P, HALF], U32, tag=tag)
-            xg_planes[a, h] = sb("xg_planes_%d_%d" % (a, h), [P, HALF], U8)
-            nc.vector.quantize_mx(xg_codes[a, h][:].bitcast(FP8X4), xg_planes[a, h][:], woven[a, h][:])
-
-        def key_passes(bank, a, h, m):
+        def key_passes(a, h, m):
             cols = slice(m * P, (m + 1) * P)
-            for part in range(2):
+            for part in (HI, LO):
                 nc.tensor.matmul_mx(
-                    bank[:],
-                    lhsT=wk_codes[a, part][:, cols].bitcast(FP8X4),
-                    lhsT_scale=wk_planes[a, part][:, cols],
-                    rhs=xg_codes[a, h][:].bitcast(FP8X4),
-                    rhs_scale=xg_planes[a, h][:],
-                    start=(a == 0 and part == 0),
-                    stop=(a == PASSES - 1 and part == 1),
+                    ke[h, m][:],
+                    lhsT=wk_mx[a, part][0][:, cols].bitcast(FP8X4),
+                    lhsT_scale=wk_mx[a, part][1][:, cols],
+                    rhs=xg_mx[a, h][0][:].bitcast(FP8X4),
+                    rhs_scale=xg_mx[a, h][1][:],
+                    start=(a == 0 and part == HI),
+                    stop=(a == PASSES - 1 and part == LO),
                 )
 
-        def value_pass(bank, a, h, m):
+        def value_pass(a, h, m):
             nc.tensor.matmul_mx(
-                bank[:],
+                ve[h, m][:],
                 lhsT=wv_codes[:, a, 2 * P * m : 2 * P * (m + 1)].bitcast(FP4X4),
-                lhsT_scale=wv_planes[:, a, P * m : P * (m + 1)],
-                rhs=xg_codes[a, h][:].bitcast(FP8X4),
-                rhs_scale=xg_planes[a, h][:],
+                lhsT_scale=wv_scale_tile[:, a, P * m : P * (m + 1)],
+                rhs=xg_mx[a, h][0][:].bitcast(FP8X4),
+                rhs_scale=xg_mx[a, h][1][:],
                 start=(a == 0),
                 stop=(a == PASSES - 1),
             )
 
-        def psum_bank(name, b):
-            return psum.tile([P, HALF], F32, name=name, tag="bank%d" % b)
+        def make_gate(h, m, gate):
+            nc.vector.tensor_tensor(gate, ke[h, m][:], st_tile[m][:, h * HALF : (h + 1) * HALF], ALU.mult)
+            nc.scalar.activation(gate, gate, ACT.Sigmoid)
+            return gate
 
-        def pick(picked, a, j0, width):
-            for t in range(PACK):
-                gather(picked[:, t, :], a, t, j0, width)
-            lo = PACK * (j0 % HALF)
-            weave(woven[a, j0 // HALF][:, lo : lo + PACK * width], picked)
+        def store(h, m, result):
+            nc.sync.dma_start(out[m * P : (m + 1) * P, h * HALF : (h + 1) * HALF], result)
 
-        woven = {(a, h): sb("xg_woven_%d_%d" % (a, h), [P, PACK * HALF], BF16) for a in range(PASSES) for h in range(2)}
+        ident = sbuf_tile("ident", [P, P], F32)
+        make_identity(nc, ident[:])
+        neg_hi_1 = sbuf_tile("neg_hi_1", [P, SLOTS, N], F32)
+        hi_0 = sbuf_tile("hi_0", [P, SLOTS, N], F32)
+        lo_0 = sbuf_tile("lo_0", [P, SLOTS, N], BF16)
+        xg_woven = {
+            (a, h): sbuf_tile("xg_woven_%d_%d" % (a, h), [P, SLOTS * HALF], BF16) for a in range(PASSES) for h in range(2)
+        }
+        wk_mx, xg_mx, ke, ve = {}, {}, {}, {}
 
-        picked_00 = sb("picked_0_0", [P, PACK, HALF], F32)
-        picked_01 = sb("picked_0_1", [P, PACK, HALF - DEFER], F32)
-        split_wk(0)
-        for t in range(PACK):
+        picked_00 = sbuf_tile("picked_0_0", [P, SLOTS, HALF], F32)
+        picked_01 = sbuf_tile("picked_0_1", [P, SLOTS, HALF], F32)
+        for pair in slot_pairs:
+            raw, hi = wk_raw[0][:, pair, :], hi_0[:, pair, :]
+            nc.vector.tensor_scalar(hi.bitcast(I32), raw.bitcast(I32), HI_MASK, None, ALU.bitwise_and)
+            nc.vector.tensor_tensor(lo_0[:, pair, :], raw, hi, ALU.subtract)
+
+        for t in range(SLOTS):
             gather(picked_00[:, t, :], 0, t, 0, HALF)
-            gather(picked_01[:, t, :], 0, t, HALF, HALF - DEFER)
-        split_wk(1)
-        quantise_wk(0, (None, None))
-        quantise_wk(1, (None, None))
-        weave(woven[0, 0][:], picked_00[:])
-        quantise_xg(0, 0)
-        weave(woven[0, 1][:, 0 : PACK * (HALF - DEFER)], picked_01[:])
-        ke = {(0, m): psum_bank("ke_0_%d" % m, m) for m in range(M_TILES)}
-        ve = {(0, m): psum_bank("ve_0_%d" % m, M_TILES + m) for m in range(M_TILES)}
-        for m in range(M_TILES):
-            key_passes(ke[0, m], 0, 0, m)
-        for m in range(M_TILES):
-            value_pass(ve[0, m], 0, 0, m)
+            gather(picked_01[:, t, :], 0, t, HALF, HALF)
 
-        picked_10 = sb("picked_1_0", [P, PACK, HALF], F32)
-        for t in range(PACK - 1):
+        nc.vector.tensor_scalar(
+            neg_hi_1[:].bitcast(I32), wk_raw[1][:].bitcast(I32), HI_MASK, SIGN_BIT, ALU.bitwise_and, ALU.bitwise_xor
+        )
+
+        hi_woven_0 = sbuf_tile("hi_woven_0", [P, SLOTS * N], BF16)
+        lo_woven_0 = sbuf_tile("lo_woven_0", [P, SLOTS * N], BF16)
+        weave(hi_woven_0[:], hi_0[:])
+        weave(lo_woven_0[:], lo_0[:])
+        wk_mx[0, HI] = quantise("wk_hi_0", hi_woven_0, tag="x_0_0")
+        wk_mx[0, LO] = quantise("wk_lo_0", lo_woven_0, tag="x_0_1")
+
+        hi_woven_1 = sbuf_tile("hi_woven_1", [P, SLOTS * N], BF16)
+        lo_woven_1 = sbuf_tile("lo_woven_1", [P, SLOTS * N], BF16)
+        nc.scalar.activation(woven_view(hi_woven_1[:]), slotted_view(neg_hi_1[:]), ACT.Copy, scale=-1.0)
+        lo_words = lo_woven_1[:].bitcast(F32)
+        for m_pair in range(M_TILES // 2):
+            back = psum_tile("back_%d" % m_pair, 6 + m_pair, [P, 2, 2, P])
+            for s in range(2):
+                m = 2 * m_pair + s
+                cols = slice(m * P, (m + 1) * P)
+                turned = psum_tile("turned_%d" % m, 4 + s, [P, SLOTS, P])
+                for t in range(SLOTS):
+                    for src, first in ((wk_raw[1], True), (neg_hi_1, False)):
+                        nc.tensor.matmul(
+                            turned[:, t, :], src[:, t, cols], ident[:], start=first, stop=not first, is_transpose=True
+                        )
+                lo_turned = sbuf_tile("lo_turned_%d" % m, [P, K_PASS], BF16)
+                nc.scalar.copy(
+                    lo_turned[:].rearrange("n (u p e) -> n u p e", u=2, e=2),
+                    turned[:].rearrange("n (u e) p -> n u p e", e=2),
+                )
+                turned_words = lo_turned[:].bitcast(F32)
+                for u in range(2):
+                    nc.tensor.transpose(back[:, s, u, :], turned_words[:, u * P : (u + 1) * P], ident[:])
+            nc.scalar.copy(
+                lo_words[:, 4 * P * m_pair : 4 * P * (m_pair + 1)].rearrange("p (s n u) -> p s n u", s=2, u=2),
+                back[:].rearrange("p s u n -> p s n u"),
+            )
+        wk_mx[1, HI] = quantise("wk_hi_1", hi_woven_1)
+        wk_mx[1, LO] = quantise("wk_lo_1", lo_woven_1, tag="x_0_3")
+
+        weave(xg_woven[0, 0][:], picked_00[:])
+        xg_mx[0, 0] = quantise("xg_0_0", xg_woven[0, 0])
+        weave(xg_woven[0, 1][:], picked_01[:])
+        for m in range(M_TILES):
+            ke[0, m] = psum_tile("ke_0_%d" % m, m, [P, HALF])
+        for m in range(M_TILES):
+            ve[0, m] = psum_tile("ve_0_%d" % m, M_TILES + m, [P, HALF])
+        for m in range(M_TILES):
+            key_passes(0, 0, m)
+        for m in range(M_TILES):
+            value_pass(0, 0, m)
+
+        picked_10 = sbuf_tile("picked_1_0", [P, SLOTS, HALF], F32)
+        for t in range(SLOTS - 1):
             gather(picked_10[:, t, :], 1, t, 0, HALF)
         for j0 in (0, QUARTER):
-            gather(picked_10[:, PACK - 1, j0 : j0 + QUARTER], 1, PACK - 1, j0, QUARTER)
-            weave(woven[1, 0][:, PACK * j0 : PACK * (j0 + QUARTER)], picked_10[:, :, j0 : j0 + QUARTER])
-        held = sb("picked_held", [P, PACK * (DEFER + LEAD)], F32, tag="wgt_0")
-        pick(held[:, 0 : PACK * DEFER].rearrange("p (t c) -> p t c", t=PACK), 0, J - DEFER, DEFER)
-        pick(held[:, PACK * DEFER :].rearrange("p (t c) -> p t c", t=PACK), 1, HALF, LEAD)
-        quantise_xg(1, 0)
-        for m in range(M_TILES):
-            value_pass(ve[0, m], 1, 0, m)
-        for m in range(M_TILES):
-            key_passes(ke[0, m], 1, 0, m)
-        quantise_xg(0, 1)
-        values = {}
-        for m in range(M_TILES):
-            values[m] = sb("values_%d" % m, [P, HALF], F32)
-            nc.scalar.copy(values[m][:], ve[0, m][:])
-            ke[1, m] = psum_bank("ke_1_%d" % m, M_TILES + m)
-            key_passes(ke[1, m], 0, 1, m)
-        picked_11 = sb("picked_1_1", [P, PACK * (HALF - LEAD)], F32, tag="xg_woven_1_0")
-        j0 = HALF + LEAD
-        for width in CHUNKS:
-            lo = PACK * (j0 - HALF - LEAD)
-            pick(picked_11[:, lo : lo + PACK * width].rearrange("p (t c) -> p t c", t=PACK), 1, j0, width)
-            j0 = j0 + width
+            gather(picked_10[:, SLOTS - 1, j0 : j0 + QUARTER], 1, SLOTS - 1, j0, QUARTER)
+            weave(xg_woven[1, 0][:, SLOTS * j0 : SLOTS * (j0 + QUARTER)], picked_10[:, :, j0 : j0 + QUARTER])
 
-        def gate_of(h, m, logits):
-            nc.vector.tensor_tensor(logits[:], ke[h, m][:], st_rows[m][:, h * HALF : (h + 1) * HALF], ALU.mult)
-            nc.scalar.activation(logits[:], logits[:], SIGMOID)
-            return logits
+        first_run = sbuf_tile("first_run", [P, SLOTS * RUN_BESIDE_WEAVE], F32, tag="wgt_0")
+        gather_and_weave(first_run[:], 1, HALF, RUN_BESIDE_WEAVE)
+        xg_mx[1, 0] = quantise("xg_1_0", xg_woven[1, 0])
+        for m in range(M_TILES):
+            value_pass(1, 0, m)
+        for m in range(M_TILES):
+            key_passes(1, 0, m)
 
-        def finish(h, m, gate, value):
-            if m < 0:
-                staged = sb("values_1_%d" % m, [P, HALF], F32)
-                nc.scalar.copy(staged[:], value[:])
-                nc.gpsimd.tensor_tensor(gate[:], staged[:], gate[:], ALU.mult)
-                nc.sync.dma_start(out[m * P : (m + 1) * P, h * HALF : (h + 1) * HALF], gate[:])
-            else:
-                step = 512 if m == M_TILES - 1 else HALF
-                for c0 in range(0, HALF, step):
-                    cols = slice(c0, c0 + step)
-                    nc.vector.tensor_tensor(gate[:, cols], value[:, cols], gate[:, cols], ALU.mult)
-                    nc.sync.dma_start(out[m * P : (m + 1) * P, h * HALF + c0 : h * HALF + c0 + step], gate[:, cols])
+        xg_mx[0, 1] = quantise("xg_0_1", xg_woven[0, 1], tag="picked_1_0")
+        values_0 = {}
+        for m in range(M_TILES):
+            values_0[m] = sbuf_tile("values_0_%d" % m, [P, HALF], F32)
+            nc.scalar.copy(values_0[m][:], ve[0, m][:])
+            ke[1, m] = psum_tile("ke_1_%d" % m, M_TILES + m, [P, HALF])
+            key_passes(0, 1, m)
 
-        quantise_xg(1, 1)
-        late = sb("late", [P, M_TILES + 2, HALF], F32, tag="xg_woven_1_1")
+        later_runs = sbuf_tile("later_runs", [P, SLOTS * sum(RUNS_AFTER_QUANTISE)], F32, tag="xg_woven_1_0")
+        done = 0
+        for width in RUNS_AFTER_QUANTISE:
+            flat = later_runs[:, SLOTS * done : SLOTS * (done + width)]
+            gather_and_weave(flat, 1, HALF + RUN_BESIDE_WEAVE + done, width)
+            done = done + width
+        xg_mx[1, 1] = quantise("xg_1_1", xg_woven[1, 1])
+
+        late = sbuf_tile("late", [P, M_TILES + GATES_BEHIND_LAST_QUANTISE, HALF], F32, tag="xg_woven_1_1")
         gates = {}
         for m in range(M_TILES):
-            if m < M_TILES - 2:
-                gates[0, m] = gate_of(0, m, sb("logits_0_%d" % m, [P, HALF], F32))
+            if m < M_TILES - GATES_BEHIND_LAST_QUANTISE:
+                gates[0, m] = make_gate(0, m, sbuf_tile("gate_0_%d" % m, [P, HALF], F32)[:])
             else:
-                gates[0, m] = gate_of(0, m, late[:, m + 2, :])
+                gates[0, m] = make_gate(0, m, late[:, m + GATES_BEHIND_LAST_QUANTISE, :])
         for m in range(M_TILES):
-            ve[1, m] = psum_bank("ve_1_%d" % m, m)
+            ve[1, m] = psum_tile("ve_1_%d" % m, m, [P, HALF])
         for m in range(M_TILES):
-            nc.gpsimd.tensor_tensor(late[:, m, :], values[m][:], gates[0, m][:], ALU.mult)
-            nc.sync.dma_start(out[m * P : (m + 1) * P, 0:HALF], late[:, m, :])
-        for m in range(M_TILES + 2):
-            if m < M_TILES:
-                key_passes(ke[1, m], 1, 1, m)
-                gates[1, m] = gate_of(1, m, sb("logits_1_%d" % m, [P, HALF], F32))
-            if m >= 2:
-                done = m - 2
+            nc.gpsimd.tensor_tensor(late[:, m, :], values_0[m][:], gates[0, m], ALU.mult)
+            store(0, m, late[:, m, :])
+        for step in range(M_TILES + FINISH_LAG):
+            if step < M_TILES:
+                key_passes(1, 1, step)
+                gates[1, step] = make_gate(1, step, sbuf_tile("gate_1_%d" % step, [P, HALF], F32)[:])
+            if step >= FINISH_LAG:
+                m = step - FINISH_LAG
                 for a in range(PASSES):
-                    value_pass(ve[1, done], a, 1, done)
-                finish(1, done, gates[1, done], ve[1, done])
+                    value_pass(a, 1, m)
+                nc.vector.tensor_tensor(gates[1, m], ve[1, m][:], gates[1, m], ALU.mult)
+                store(1, m, gates[1, m])

@@ -195,11 +195,11 @@ def tile_list_hl_sig_kernel(tc, xT, wgt, wk, wv_words, wv_scales, st, offs, out)
         nc.scalar.activation(woven_view(hi_woven_1[:]), slotted_view(neg_hi_1[:]), ACT.Copy, scale=-1.0)
         lo_words = lo_woven_1[:].bitcast(F32)
         for m_pair in range(M_TILES // 2):
-            back = psum_tile("back_%d" % m_pair, 6 + m_pair, [P, 2, 2, P])
+            back = psum_tile("back_%d" % m_pair, M_TILES + m_pair, [P, 2, 2, P])
             for s in range(2):
                 m = 2 * m_pair + s
                 cols = slice(m * P, (m + 1) * P)
-                turned = psum_tile("turned_%d" % m, 4 + s, [P, SLOTS, P])
+                turned = psum_tile("turned_%d" % m, m, [P, SLOTS, P])
                 for t in range(SLOTS):
                     for src, first in ((wk_raw[1], True), (neg_hi_1, False)):
                         nc.tensor.matmul(

from contextlib import ExitStack

import concourse.mybir as mybir
from concourse.masks import make_identity

K, N, T, J = 1024, 512, 2048, 1024
FLOPS = 3 * 2 * K * N * J

F32 = mybir.dt.float32
BF16 = mybir.dt.bfloat16
I32 = mybir.dt.int32
U32 = mybir.dt.uint32
U16 = mybir.dt.uint16
U8 = mybir.dt.uint8
FP8X4 = mybir.dt.float8_e4m3fn_x4
FP4X4 = mybir.dt.float4_e2m1fn_x4
ALU = mybir.AluOpType
ACT = mybir.ActivationFunctionType

P = 128
SLOTS = 4
K_PASS = P * SLOTS
PASSES = K // K_PASS
HALF = 512
QUARTER = HALF // 2
M_TILES = N // P
LIST_ROWS = 16
HI, LO = 0, 1

HI_MASK = 0xFFF00000 - (1 << 32)
SIGN_BIT = -(1 << 31)

RUN_BESIDE_WEAVE = 192
RUNS_AFTER_QUANTISE = (192, 128)
GATES_BEHIND_LAST_QUANTISE = 2
FINISH_LAG = 2


def tile_list_hl_sig_kernel(tc, xT, wgt, wk, wv_words, wv_scales, st, offs, out):
    nc = tc.nc
    with ExitStack() as ctx:
        keep = ctx.enter_context(tc.tile_pool(name="keep", bufs=1))
        psum = ctx.enter_context(tc.psum_pool(name="psum", bufs=1))

        def sbuf_tile(name, shape, dtype, tag=None):
            return keep.tile(shape, dtype, name=name, tag=tag or name, align_bytes=64)

        def psum_tile(name, bank, shape):
            return psum.tile(shape, F32, name=name, tag="bank%d" % bank)

        lists = keep.tile([P, J // LIST_ROWS], U16, name="lists")

        warm = sbuf_tile("warm", [P, 2], F32)
        nc.vector.memset(warm[:, 0:1], 0.0)
        nc.scalar.activation(warm[:, 1:2], warm[:, 0:1], ACT.Sigmoid)

        wv_scale_tile = sbuf_tile("wv_scale_tile", [P, PASSES, N], U8)
        nc.vector.memset(wv_scale_tile[:].bitcast(I32), 0)

        x_rows = xT.rearrange("(a p t) c -> a t p c", a=PASSES, t=SLOTS)
        wk_rows = wk.rearrange("(a p t) n -> a p t n", a=PASSES, t=SLOTS)
        x_tile = {}
        wk_raw = {a: sbuf_tile("wk_raw_%d" % a, [P, SLOTS, N], F32) for a in range(PASSES)}
        wgt_half = {}
        slot_pairs = (slice(0, 2), slice(2, 4))

        def load_x(a, t):
            x_tile[a, t] = sbuf_tile("x_%d_%d" % (a, t), [P, T], F32)
            nc.sync.dma_start(x_tile[a, t][:], x_rows[a, t])

        def load_wgt(h):
            wgt_half[h] = sbuf_tile("wgt_%d" % h, [P, HALF], F32)
            nc.sync.dma_start(wgt_half[h][:], wgt[:, h * HALF : (h + 1) * HALF])

        nc.sync.dma_start(wk_raw[0][:, slot_pairs[0], :], wk_rows[0, :, slot_pairs[0], :])
        nc.sync.dma_start(lists[:], offs)
        nc.sync.dma_start(wk_raw[0][:, slot_pairs[1], :], wk_rows[0, :, slot_pairs[1], :])
        load_wgt(0)
        load_x(0, 0)
        load_wgt(1)
        nc.sync.dma_start(wk_raw[1][:], wk_rows[1])
        for k_tile in range(1, PASSES * SLOTS):
            load_x(*divmod(k_tile, SLOTS))

        wv_codes = sbuf_tile("wv_codes", [P, PASSES, 2 * N], U8)
        nc.sync.dma_start(wv_codes[:].bitcast(I32), wv_words.rearrange("a p b -> p a b").bitcast(I32))
        for quadrant in range(4):
            nc.sync.dma_start(
                wv_scale_tile[32 * quadrant : 32 * quadrant + 4, :, :].bitcast(I32),
                wv_scales[:, 4 * quadrant : 4 * quadrant + 4, :].rearrange("a r n -> r a n").bitcast(I32),
            )
        st_tile = {}
        for m in range(M_TILES):
            st_tile[m] = sbuf_tile("st_%d" % m, [P, J], F32)
            nc.sync.dma_start(st_tile[m][:], st[m * P : (m + 1) * P, :])

        def woven_view(dst):
            return dst.rearrange("p (c i t) -> p c t i", i=4, t=SLOTS)

        def slotted_view(src):
            return src.rearrange("p t (c i) -> p c t i", i=4)

        def weave(dst, src):
            nc.scalar.copy(woven_view(dst), slotted_view(src))

        def quantise(name, woven_tile, tag=None):
            width = woven_tile.shape[1] // SLOTS
            codes = sbuf_tile(name + "_codes", [P, width], U32, tag=tag)
            scales = sbuf_tile(name + "_scales", [P, width], U8)
            nc.vector.quantize_mx(codes[:].bitcast(FP8X4), scales[:], woven_tile[:])
            return codes, scales

        def gather(dst, a, t, j0, width):
            h, c0 = divmod(j0, HALF)
            nc.vector.tensor_tensor(
                dst,
                x_tile[a, t][:].indirect(lists[:, j0 // LIST_ROWS : (j0 + width) // LIST_ROWS]),
                wgt_half[h][:, c0 : c0 + width],
                ALU.mult,
            )

        def gather_and_weave(flat, a, j0, width):
            picked = flat.rearrange("p (t c) -> p t c", t=SLOTS)
            for t in range(SLOTS):
                gather(picked[:, t, :], a, t, j0, width)
            h, c0 = divmod(j0, HALF)
            weave(xg_woven[a, h][:, SLOTS * c0 : SLOTS * (c0 + width)], picked)

        def key_passes(a, h, m):
            cols = slice(m * P, (m + 1) * P)
            for part in (HI, LO):
                nc.tensor.matmul_mx(
                    ke[h, m][:],
                    lhsT=wk_mx[a, part][0][:, cols].bitcast(FP8X4),
                    lhsT_scale=wk_mx[a, part][1][:, cols],
                    rhs=xg_mx[a, h][0][:].bitcast(FP8X4),
                    rhs_scale=xg_mx[a, h][1][:],
                    start=(a == 0 and part == HI),
                    stop=(a == PASSES - 1 and part == LO),
                )

        def value_pass(a, h, m):
            nc.tensor.matmul_mx(
                ve[h, m][:],
                lhsT=wv_codes[:, a, 2 * P * m : 2 * P * (m + 1)].bitcast(FP4X4),
                lhsT_scale=wv_scale_tile[:, a, P * m : P * (m + 1)],
                rhs=xg_mx[a, h][0][:].bitcast(FP8X4),
                rhs_scale=xg_mx[a, h][1][:],
                start=(a == 0),
                stop=(a == PASSES - 1),
            )

        def make_gate(h, m, gate):
            nc.vector.tensor_tensor(gate, ke[h, m][:], st_tile[m][:, h * HALF : (h + 1) * HALF], ALU.mult)
            nc.scalar.activation(gate, gate, ACT.Sigmoid)
            return gate

        def store(h, m, result):
            nc.sync.dma_start(out[m * P : (m + 1) * P, h * HALF : (h + 1) * HALF], result)

        ident = sbuf_tile("ident", [P, P], F32)
        make_identity(nc, ident[:])
        neg_hi_1 = sbuf_tile("neg_hi_1", [P, SLOTS, N], F32)
        hi_0 = sbuf_tile("hi_0", [P, SLOTS, N], F32)
        lo_0 = sbuf_tile("lo_0", [P, SLOTS, N], BF16)
        xg_woven = {
            (a, h): sbuf_tile("xg_woven_%d_%d" % (a, h), [P, SLOTS * HALF], BF16) for a in range(PASSES) for h in range(2)
        }
        wk_mx, xg_mx, ke, ve = {}, {}, {}, {}

        picked_00 = sbuf_tile("picked_0_0", [P, SLOTS, HALF], F32)
        picked_01 = sbuf_tile("picked_0_1", [P, SLOTS, HALF], F32)
        for pair in slot_pairs:
            raw, hi = wk_raw[0][:, pair, :], hi_0[:, pair, :]
            nc.vector.tensor_scalar(hi.bitcast(I32), raw.bitcast(I32), HI_MASK, None, ALU.bitwise_and)
            nc.vector.tensor_tensor(lo_0[:, pair, :], raw, hi, ALU.subtract)

        for t in range(SLOTS):
            gather(picked_00[:, t, :], 0, t, 0, HALF)
            gather(picked_01[:, t, :], 0, t, HALF, HALF)

        nc.vector.tensor_scalar(
            neg_hi_1[:].bitcast(I32), wk_raw[1][:].bitcast(I32), HI_MASK, SIGN_BIT, ALU.bitwise_and, ALU.bitwise_xor
        )

        hi_woven_0 = sbuf_tile("hi_woven_0", [P, SLOTS * N], BF16)
        lo_woven_0 = sbuf_tile("lo_woven_0", [P, SLOTS * N], BF16)
        weave(hi_woven_0[:], hi_0[:])
        weave(lo_woven_0[:], lo_0[:])
        wk_mx[0, HI] = quantise("wk_hi_0", hi_woven_0, tag="x_0_0")
        wk_mx[0, LO] = quantise("wk_lo_0", lo_woven_0, tag="x_0_1")

        hi_woven_1 = sbuf_tile("hi_woven_1", [P, SLOTS * N], BF16)
        lo_woven_1 = sbuf_tile("lo_woven_1", [P, SLOTS * N], BF16)
        nc.scalar.activation(woven_view(hi_woven_1[:]), slotted_view(neg_hi_1[:]), ACT.Copy, scale=-1.0)
        lo_words = lo_woven_1[:].bitcast(F32)
        for m_pair in range(M_TILES // 2):
            back = psum_tile("back_%d" % m_pair, M_TILES + m_pair, [P, 2, 2, P])
            for s in range(2):
                m = 2 * m_pair + s
                cols = slice(m * P, (m + 1) * P)
                turned = psum_tile("turned_%d" % m, m, [P, SLOTS, P])
                for t in range(SLOTS):
                    for src, first in ((wk_raw[1], True), (neg_hi_1, False)):
                        nc.tensor.matmul(
                            turned[:, t, :], src[:, t, cols], ident[:], start=first, stop=not first, is_transpose=True
                        )
                lo_turned = sbuf_tile("lo_turned_%d" % m, [P, K_PASS], BF16)
                nc.scalar.copy(
                    lo_turned[:].rearrange("n (u p e) -> n u p e", u=2, e=2),
                    turned[:].rearrange("n (u e) p -> n u p e", e=2),
                )
                turned_words = lo_turned[:].bitcast(F32)
                for u in range(2):
                    nc.tensor.transpose(back[:, s, u, :], turned_words[:, u * P : (u + 1) * P], ident[:])
            nc.scalar.copy(
                lo_words[:, 4 * P * m_pair : 4 * P * (m_pair + 1)].rearrange("p (s n u) -> p s n u", s=2, u=2),
                back[:].rearrange("p s u n -> p s n u"),
            )
        wk_mx[1, HI] = quantise("wk_hi_1", hi_woven_1)
        wk_mx[1, LO] = quantise("wk_lo_1", lo_woven_1, tag="x_0_3")

        weave(xg_woven[0, 0][:], picked_00[:])
        xg_mx[0, 0] = quantise("xg_0_0", xg_woven[0, 0])
        weave(xg_woven[0, 1][:], picked_01[:])
        for m in range(M_TILES):
            ke[0, m] = psum_tile("ke_0_%d" % m, m, [P, HALF])
        for m in range(M_TILES):
            ve[0, m] = psum_tile("ve_0_%d" % m, M_TILES + m, [P, HALF])
        for m in range(M_TILES):
            key_passes(0, 0, m)
        for m in range(M_TILES):
            value_pass(0, 0, m)

        picked_10 = sbuf_tile("picked_1_0", [P, SLOTS, HALF], F32)
        for t in range(SLOTS - 1):
            gather(picked_10[:, t, :], 1, t, 0, HALF)
        for j0 in (0, QUARTER):
            gather(picked_10[:, SLOTS - 1, j0 : j0 + QUARTER], 1, SLOTS - 1, j0, QUARTER)
            weave(xg_woven[1, 0][:, SLOTS * j0 : SLOTS * (j0 + QUARTER)], picked_10[:, :, j0 : j0 + QUARTER])

        first_run = sbuf_tile("first_run", [P, SLOTS * RUN_BESIDE_WEAVE], F32, tag="wgt_0")
        gather_and_weave(first_run[:], 1, HALF, RUN_BESIDE_WEAVE)
        xg_mx[1, 0] = quantise("xg_1_0", xg_woven[1, 0])
        for m in range(M_TILES):
            value_pass(1, 0, m)
        for m in range(M_TILES):
            key_passes(1, 0, m)

        xg_mx[0, 1] = quantise("xg_0_1", xg_woven[0, 1], tag="picked_1_0")
        values_0 = {}
        for m in range(M_TILES):
            values_0[m] = sbuf_tile("values_0_%d" % m, [P, HALF], F32)
            nc.scalar.copy(values_0[m][:], ve[0, m][:])
            ke[1, m] = psum_tile("ke_1_%d" % m, M_TILES + m, [P, HALF])
            key_passes(0, 1, m)

        later_runs = sbuf_tile("later_runs", [P, SLOTS * sum(RUNS_AFTER_QUANTISE)], F32, tag="xg_woven_1_0")
        done = 0
        for width in RUNS_AFTER_QUANTISE:
            flat = later_runs[:, SLOTS * done : SLOTS * (done + width)]
            gather_and_weave(flat, 1, HALF + RUN_BESIDE_WEAVE + done, width)
            done = done + width
        xg_mx[1, 1] = quantise("xg_1_1", xg_woven[1, 1])

        late = sbuf_tile("late", [P, M_TILES + GATES_BEHIND_LAST_QUANTISE, HALF], F32, tag="xg_woven_1_1")
        gates = {}
        for m in range(M_TILES):
            if m < M_TILES - GATES_BEHIND_LAST_QUANTISE:
                gates[0, m] = make_gate(0, m, sbuf_tile("gate_0_%d" % m, [P, HALF], F32)[:])
            else:
                gates[0, m] = make_gate(0, m, late[:, m + GATES_BEHIND_LAST_QUANTISE, :])
        for m in range(M_TILES):
            ve[1, m] = psum_tile("ve_1_%d" % m, m, [P, HALF])
        for m in range(M_TILES):
            nc.gpsimd.tensor_tensor(late[:, m, :], values_0[m][:], gates[0, m], ALU.mult)
            store(0, m, late[:, m, :])
        for step in range(M_TILES + FINISH_LAG):
            if step < M_TILES:
                key_passes(1, 1, step)
                gates[1, step] = make_gate(1, step, sbuf_tile("gate_1_%d" % step, [P, HALF], F32)[:])
            if step >= FINISH_LAG:
                m = step - FINISH_LAG
                for a in range(PASSES):
                    value_pass(a, 1, m)
                nc.vector.tensor_tensor(gates[1, m], ve[1, m][:], gates[1, m], ALU.mult)
                store(1, m, gates[1, m])
